import numpy as np
import ml_dtypes


def mxq(x, axis, fmt="e4m3"):
    dtype, down = {"e4m3": (ml_dtypes.float8_e4m3fn, 7), "e5m2": (ml_dtypes.float8_e5m2, 14)}[fmt]
    v = np.moveaxis(np.asarray(x, np.float32).astype(ml_dtypes.bfloat16).astype(np.float64), axis, -1)
    blocks = v.reshape(v.shape[:-1] + (-1, 32))
    amax = np.abs(blocks).max(-1, keepdims=True)
    byte = np.maximum(np.where(amax > 0, np.frexp(amax)[1] - 1 + 127, 0) - down, 1)
    scale = np.exp2(byte - 127.0)
    codes = (blocks / scale).astype(np.float32).astype(dtype).astype(np.float64)
    return np.moveaxis((codes * scale).reshape(v.shape), -1, axis)


WIDE = False


def mx_kscale(k):
    if not WIDE:
        return np.ones(k)
    levels = np.array([10, -10, 5, -5, 0])
    if k % 512:
        return np.exp2(np.random.permutation(np.resize(levels, k // 32))).repeat(32)
    a = np.empty((k // 512, 16))
    for p in range(k // 512):
        a[p, :8] = np.random.permutation(np.resize(levels, 8))
        for g in range(8):
            far = levels[np.abs(levels - a[p, g]) >= 10]
            a[p, g + 8] = far[np.random.randint(len(far))]
    return np.exp2(a.ravel()).repeat(32)


def f64(x):
    return np.asarray(x).astype(np.float64)


def striped(idx):
    return np.tile(idx.reshape(-1, 16).T, (8, 1)).astype(np.uint16)


def unstriped(offs):
    return offs[:16].T.reshape(-1).astype(np.int64)


def relu(v):
    return np.maximum(v, 0.0)


K, T, E, C, H, N = 512, 1536, 6, 128, 1024, 512


def by_expert(wq, xq):
    return np.concatenate([wq[e].T @ xq[:, e * C:(e + 1) * C] for e in range(E)], axis=1)


def setup_inputs():
    n = np.random.standard_normal
    s = mx_kscale(K)[:, None]
    u = mx_kscale(H)
    return {
        "xT": (n((K, T)) * s).astype(np.float32),
        "w1": (n((E, K, H)) / np.sqrt(K) / s[None] * u[None, None, :]).astype(np.float32),
        "w2": (n((E, H, N)) / np.sqrt(H) / u[None, :, None]).astype(np.float32),
        "gate": np.tile(np.random.uniform(0.2, 1.0, E * C), (N, 1)).astype(np.float32),
        "offs": striped(np.random.permutation(T)[:E * C]),
    }


def reference(xT, w1, w2, gate, offs):
    idx = unstriped(offs)
    xq = mxq(f64(xT)[:, idx], 0, "e4m3")
    h = relu(by_expert(mxq(f64(w1), 1, "e4m3"), xq))
    y = by_expert(mxq(f64(w2), 1, "e4m3"), mxq(h, 0, "e4m3"))
    out = np.zeros((N, T))
    out[:, idx] = f64(gate) * y
    return out

@@ -1,0 +1,228 @@
+import concourse.mybir as mybir
+
+F32 = mybir.dt.float32
+BF16 = mybir.dt.bfloat16
+U32 = mybir.dt.uint32
+U16 = mybir.dt.uint16
+U8 = mybir.dt.uint8
+FP8X4 = mybir.dt.float8_e4m3fn_x4
+RELU = mybir.ActivationFunctionType.Relu
+MULT = mybir.AluOpType.mult
+
+P = 128
+K, T, E, C, H, N = 512, 1536, 6, 128, 1024, 512
+S = E * C
+FLOPS = 2 * S * (K * H + H * N)
+
+UNIT = 512
+X_VEC = 256
+W1_VEC = 32
+W2_VEC = 64
+CUT = 192
+NB = N // P
+
+
+def tile_routed_moe_kernel(tc, xT, w1, w2, gate, offs, out):
+    nc = tc.nc
+    x_view = xT.rearrange("(p j) t -> p j t", j=4)
+    w1_view = w1.rearrange("e (p j) i -> e p j i", j=4)
+    w2_view = w2.rearrange("e (g p j) n -> e p g (j n)", g=2, j=4)
+    w2_rows = w2.rearrange("e (g p j) n -> e g p j n", g=2, j=4)
+    gate_view = gate.rearrange("(b p) s -> p b s", p=P)
+
+    with (
+        tc.tile_pool(name="keep", bufs=1) as keep,
+        tc.tile_pool(name="ring", bufs=5) as ring,
+        tc.tile_pool(name="tail", bufs=4) as tail,
+        tc.tile_pool(name="stage", bufs=6) as stage,
+        tc.tile_pool(name="codes", bufs=8) as codes,
+        tc.tile_pool(name="hidden", bufs=3) as hidden,
+        tc.psum_pool(name="psum_h", bufs=4) as psum_h,
+        tc.psum_pool(name="psum_y", bufs=4) as psum_y,
+    ):
+        lists = keep.tile([P, S // 16], U16, name="lists")
+        x_words = keep.tile([P, T], U32, name="x_words", align_bytes=64)
+        x_bytes = keep.tile([P, T], U8, name="x_bytes", align_bytes=64)
+        s_words = keep.tile([P, S], U32, name="s_words", align_bytes=64)
+        s_bytes = keep.tile([P, S], U8, name="s_bytes", align_bytes=64)
+        gates = keep.tile([P, NB, S], F32, name="gates")
+        y = keep.tile([P, NB, S], F32, name="y")
+        windows = []
+        for b in range(NB):
+            window = keep.tile([P, T], F32, name="window%d" % b)
+            windows.append(window)
+
+        nc.sync.dma_start(lists[:], offs)
+        for b in range(NB):
+            nc.vector.memset(windows[b][:], 0.0)
+
+        raw_x, raw_w1, raw_w2, raw_q = {}, {}, {}, {}
+
+        def load_x(c):
+            raw = ring.tile([P, 4 * UNIT], F32, name="raw")
+            nc.sync.dma_start(raw[:].rearrange("p (j t) -> p j t", j=4), x_view[:, :, c * UNIT:(c + 1) * UNIT])
+            raw_x[c] = raw[:].rearrange("p (j t) -> p j t", j=4)
+
+        def load_w1(e):
+            raw = ring.tile([P, 4 * H], F32, name="raw")
+            nc.sync.dma_start(raw[:].rearrange("p (j i) -> p j i", j=4), w1_view[e, :, :, :])
+            raw_w1[e] = raw[:].rearrange("p (j i) -> p j i", j=4)
+
+        def load_w2(e):
+            raw = ring.tile([P, 2 * 4 * N], F32, name="raw")
+            nc.sync.dma_start(raw[:].rearrange("p (g r) -> p g r", g=2), w2_view[e, :, :, :])
+            raw_w2[e] = raw[:].rearrange("p (g j n) -> p g j n", g=2, j=4)
+
+        def load_q(b):
+            raw = tail.tile([P, 2, 4, P], F32, name="raw_q")
+            for g in range(2):
+                nc.sync.dma_start(raw[:, g, :, :], w2_rows[E - 1, g, :, :, b * P:(b + 1) * P])
+            raw_q[b] = raw
+
+        grouped = {}
+        quantised = {}
+        sums = {}
+        hid = {}
+        h_codes = {}
+
+        def interleave(copy, dst, src, lo, hi):
+            d = dst[:, 4 * lo:4 * hi].rearrange("p (c i j) -> p c j i", i=4, j=4)
+            s = src[:, :, lo:hi].rearrange("p j (c i) -> p c j i", i=4)
+            copy(out=d, in_=s)
+
+        def copy_unit(u):
+            kind, a, b = u
+            if kind == "q":
+                g_tile = stage.tile([P, 2 * 4 * P], BF16, name="grouped", align_bytes=64)
+                for g in range(2):
+                    d = g_tile[:, g * 4 * P:(g + 1) * 4 * P]
+                    interleave(nc.scalar.copy, d, raw_q[a][:, g, :, :], 0, P)
+            else:
+                g_tile = stage.tile([P, 4 * UNIT], BF16, name="grouped", align_bytes=64)
+                if kind == "x":
+                    cut = UNIT - X_VEC
+                    interleave(nc.scalar.copy, g_tile[:], raw_x[a], 0, cut)
+                    interleave(nc.vector.tensor_copy, g_tile[:], raw_x[a], cut, UNIT)
+                elif kind == "w2":
+                    cut = UNIT - W2_VEC
+                    interleave(nc.scalar.copy, g_tile[:], raw_w2[a][:, b, :, :], 0, cut)
+                    interleave(nc.vector.tensor_copy, g_tile[:], raw_w2[a][:, b, :, :], cut, UNIT)
+                else:
+                    src = raw_w1[a][:, :, b * UNIT:(b + 1) * UNIT].rearrange("p j (m t) -> p m j t", t=4)
+                    dst = g_tile[:].rearrange("p (t m j) -> p m j t", t=4, j=4)
+                    cut = P - W1_VEC
+                    nc.scalar.copy(out=dst[:, :cut, :, :], in_=src[:, :cut, :, :])
+                    nc.vector.tensor_copy(out=dst[:, cut:, :, :], in_=src[:, cut:, :, :])
+            grouped[u] = g_tile
+
+        def quantise_unit(u):
+            kind, a, b = u
+            if kind == "x":
+                cols = slice(a * UNIT, (a + 1) * UNIT)
+                nc.vector.quantize_mx(out=x_words[:, cols].bitcast(FP8X4), scales=x_bytes[:, cols], in_=grouped[u][:])
+                return
+            width = 2 * P if kind == "q" else UNIT
+            words = codes.tile([P, width], U32, name="words", align_bytes=64)
+            scales = codes.tile([P, width], U8, name="scales", align_bytes=64)
+            nc.vector.quantize_mx(out=words[:].bitcast(FP8X4), scales=scales[:], in_=grouped[u][:])
+            quantised[u] = (words, scales)
+
+        def mx(dst, weights, cols, right, right_scale, start, stop):
+            words, scales = weights
+            nc.tensor.matmul_mx(out=dst, lhsT=words[:, cols].bitcast(FP8X4), lhsT_scale=scales[:, cols],
+                                rhs=right.bitcast(FP8X4), rhs_scale=right_scale, start=start, stop=stop)
+
+        def multiply_unit(u):
+            kind, a, b = u
+            if kind == "x":
+                if a == T // UNIT - 1:
+                    nc.vector.tensor_copy(s_words[:], x_words[:].indirect(lists[:]))
+                    nc.vector.tensor_copy(s_bytes[:], x_bytes[:].indirect(lists[:]))
+            elif kind == "w1":
+                acc = psum_h.tile([P, 4, C], F32, name="acc_h")
+                slots = slice(a * C, (a + 1) * C)
+                for t in range(4):
+                    mx(acc[:, t, :], quantised[u], slice(t * P, (t + 1) * P), s_words[:, slots], s_bytes[:, slots], True, True)
+                h = hidden.tile([P, C, 4], BF16, name="h", align_bytes=64)
+                nc.scalar.activation(out=h[:], in_=acc[:].rearrange("p t s -> p s t"), func=RELU)
+                hid[u] = h
+            elif kind == "w2" and b == 1:
+                acc = psum_y.tile([P, NB, C], F32, name="acc_y")
+                for n in range(NB):
+                    for g in range(2):
+                        hw, hs = h_codes[a, g]
+                        mx(acc[:, n, :], quantised["w2", a, g], slice(n * P, (n + 1) * P), hw[:], hs[:], g == 0, g == 1)
+                sums[u] = acc
+            elif kind == "q":
+                acc = psum_y.tile([P, C], F32, name="acc_y")
+                for g in range(2):
+                    hw, hs = h_codes[E - 1, g]
+                    mx(acc[:], quantised[u], slice(g * P, (g + 1) * P), hw[:], hs[:], g == 0, g == 1)
+                sums[u] = acc
+
+        def scatter(b, k):
+            nc.vector.tensor_tensor(windows[b][:].indirect(lists[:, k * CUT // 16:(k + 1) * CUT // 16]), y[:, b, k * CUT:(k + 1) * CUT], gates[:, b, k * CUT:(k + 1) * CUT], MULT)
+
+        def finish_unit(u):
+            kind, a, b = u
+            if kind == "w1":
+                hw = hidden.tile([P, C], U32, name="h_words%d" % b, align_bytes=64)
+                hs = hidden.tile([P, C], U8, name="h_scales%d" % b, align_bytes=64)
+                nc.vector.quantize_mx(out=hw[:].bitcast(FP8X4), scales=hs[:], in_=hid[u][:].rearrange("p s t -> p (s t)"))
+                h_codes[a, b] = (hw, hs)
+            elif kind == "w2" and b == 1:
+                slots = slice(a * C, (a + 1) * C)
+                nc.scalar.copy(out=y[:, :, slots], in_=sums[u][:])
+                for k in range(S // CUT):
+                    if a * C < (k + 1) * CUT <= (a + 1) * C:
+                        for n in range(NB):
+                            scatter(n, k)
+            elif kind == "q":
+                slots = slice(S - C, S)
+                nc.scalar.copy(out=y[:, a, slots], in_=sums[u][:])
+                scatter(a, S // CUT - 1)
+                nc.sync.dma_start(out[a * P:(a + 1) * P, :], windows[a][:])
+
+        units = [("x", c, 0) for c in range(T // UNIT)]
+        items = [(load_x, c) for c in range(T // UNIT)]
+        for e in range(E):
+            items.append((load_w1, e))
+            units.extend([("w1", e, 0), ("w1", e, 1)])
+            if e < E - 1:
+                items.append((load_w2, e))
+                units.extend([("w2", e, 0), ("w2", e, 1)])
+        items.extend([(load_q, b) for b in range(NB)])
+        units.extend([("q", b, 0) for b in range(NB)])
+
+        issued = 0
+
+        def issue(upto):
+            done = issued
+            while done < min(upto, len(items)):
+                load, arg = items[done]
+                load(arg)
+                done += 1
+                if done == 4:
+                    nc.sync.dma_start(gates[:], gate_view)
+            return done
+
+        first_item = {}
+        for u in units:
+            if u[0] == "x":
+                first_item[u] = u[1]
+            elif u[0] == "q":
+                first_item[u] = len(items) - NB + u[1]
+            else:
+                first_item[u] = 3 + 2 * u[1] + (0 if u[0] == "w1" else 1)
+        AHEAD = 5
+        for step in range(len(units) + 3):
+            if step < len(units):
+                issued = issue(first_item[units[step]] + AHEAD)
+            if 3 <= step:
+                finish_unit(units[step - 3])
+            if 2 <= step < len(units) + 2:
+                multiply_unit(units[step - 2])
+            if 1 <= step < len(units) + 1:
+                quantise_unit(units[step - 1])
+            if step < len(units):
+                copy_unit(units[step])

@@ -7,7 +7,11 @@ U16 = mybir.dt.uint16
 U8 = mybir.dt.uint8
 FP8X4 = mybir.dt.float8_e4m3fn_x4
 RELU = mybir.ActivationFunctionType.Relu
+IDENTITY = mybir.ActivationFunctionType.Identity
 MULT = mybir.AluOpType.mult
+ADD = mybir.AluOpType.add
+MAX = mybir.AluOpType.max
+MIN = mybir.AluOpType.min
 
 P = 128
 K, T, E, C, H, N = 512, 1536, 6, 128, 1024, 512
@@ -15,10 +19,9 @@ S = E * C
 FLOPS = 2 * S * (K * H + H * N)
 
 UNIT = 512
-X_VEC = 256
-W1_VEC = 32
-W2_VEC = 64
-CUT = 192
+AHEAD = 11
+LAST = 2
+CUT = 256
 NB = N // P
 
 
@@ -26,17 +29,17 @@ def tile_routed_moe_kernel(tc, xT, w1, w2, gate, offs, out):
     nc = tc.nc
     x_view = xT.rearrange("(p j) t -> p j t", j=4)
     w1_view = w1.rearrange("e (p j) i -> e p j i", j=4)
-    w2_view = w2.rearrange("e (g p j) n -> e p g (j n)", g=2, j=4)
+    w2_view = w2.rearrange("e (g p j) n -> e g p (j n)", g=2, j=4)
     w2_rows = w2.rearrange("e (g p j) n -> e g p j n", g=2, j=4)
     gate_view = gate.rearrange("(b p) s -> p b s", p=P)
 
     with (
         tc.tile_pool(name="keep", bufs=1) as keep,
-        tc.tile_pool(name="ring", bufs=5) as ring,
-        tc.tile_pool(name="tail", bufs=4) as tail,
-        tc.tile_pool(name="stage", bufs=6) as stage,
-        tc.tile_pool(name="codes", bufs=8) as codes,
+        tc.tile_pool(name="ring", bufs=AHEAD) as ring,
+        tc.tile_pool(name="stage", bufs=8) as stage,
+        tc.tile_pool(name="codes", bufs=9) as codes,
         tc.tile_pool(name="hidden", bufs=3) as hidden,
+        tc.tile_pool(name="tokens", bufs=16) as tokens,
         tc.psum_pool(name="psum_h", bufs=4) as psum_h,
         tc.psum_pool(name="psum_y", bufs=4) as psum_y,
     ):
@@ -54,65 +57,76 @@ def tile_routed_moe_kernel(tc, xT, w1, w2, gate, offs, out):
 
         nc.sync.dma_start(lists[:], offs)
         for b in range(NB):
-            nc.vector.memset(windows[b][:], 0.0)
+            engine = nc.gpsimd
+            engine.memset(windows[b][:], 0.0)
 
-        raw_x, raw_w1, raw_w2, raw_q = {}, {}, {}, {}
-
-        def load_x(c):
-            raw = ring.tile([P, 4 * UNIT], F32, name="raw")
-            nc.sync.dma_start(raw[:].rearrange("p (j t) -> p j t", j=4), x_view[:, :, c * UNIT:(c + 1) * UNIT])
-            raw_x[c] = raw[:].rearrange("p (j t) -> p j t", j=4)
-
-        def load_w1(e):
-            raw = ring.tile([P, 4 * H], F32, name="raw")
-            nc.sync.dma_start(raw[:].rearrange("p (j i) -> p j i", j=4), w1_view[e, :, :, :])
-            raw_w1[e] = raw[:].rearrange("p (j i) -> p j i", j=4)
-
-        def load_w2(e):
-            raw = ring.tile([P, 2 * 4 * N], F32, name="raw")
-            nc.sync.dma_start(raw[:].rearrange("p (g r) -> p g r", g=2), w2_view[e, :, :, :])
-            raw_w2[e] = raw[:].rearrange("p (g j n) -> p g j n", g=2, j=4)
-
-        def load_q(b):
-            raw = tail.tile([P, 2, 4, P], F32, name="raw_q")
-            for g in range(2):
-                nc.sync.dma_start(raw[:, g, :, :], w2_rows[E - 1, g, :, :, b * P:(b + 1) * P])
-            raw_q[b] = raw
-
+        raw = {}
         grouped = {}
         quantised = {}
         sums = {}
         hid = {}
         h_codes = {}
 
-        def interleave(copy, dst, src, lo, hi):
-            d = dst[:, 4 * lo:4 * hi].rearrange("p (c i j) -> p c j i", i=4, j=4)
-            s = src[:, :, lo:hi].rearrange("p j (c i) -> p c j i", i=4)
-            copy(out=d, in_=s)
+        units = [("x", c, 0) for c in range(T // UNIT)]
+        for e in range(E):
+            units.extend([("w1", e, 0), ("w1", e, 1)])
+            if e < E - LAST:
+                units.extend([("w2", e, 0), ("w2", e, 1)])
+        units.extend([("q", b, 0) for b in range(NB)])
+
+        def load(u):
+            kind, a, b = u
+            tile = ring.tile([P, 4 * UNIT], F32, name="raw")
+            if kind == "q":
+                view = tile[:, :2 * LAST * 4 * P].rearrange("p (i j n) -> p i j n", i=2 * LAST, j=4)
+                for i in range(2 * LAST):
+                    e, g = divmod(i, 2)
+                    nc.sync.dma_start(view[:, i, :, :], w2_rows[E - LAST + e, g, :, :, a * P:(a + 1) * P])
+            else:
+                view = tile[:].rearrange("p (j c) -> p j c", j=4)
+                if kind == "x":
+                    nc.sync.dma_start(view, x_view[:, :, a * UNIT:(a + 1) * UNIT])
+                elif kind == "w1":
+                    nc.sync.dma_start(view, w1_view[a, :, :, b * UNIT:(b + 1) * UNIT])
+                else:
+                    nc.sync.dma_start(tile[:], w2_view[a, b, :, :])
+            raw[u] = (tile, view)
+
+        def token(u, later):
+            at = units.index(u) + later
+            if later == 0 or at >= len(units):
+                return None
+            zero = tokens.tile([P, 1], F32, name="zero")
+            nc.gpsimd.tensor_scalar(out=zero[:], in0=raw[units[at]][0][:, 0:1], scalar1=0.0, scalar2=0.0, op0=MAX, op1=MIN)
+            return zero
+
+        def interleave(copy, dst, src):
+            copy(out=dst.rearrange("p (c i j) -> p c j i", i=4, j=4), in_=src.rearrange("p j (c i) -> p c j i", i=4))
 
         def copy_unit(u):
             kind, a, b = u
+            view = raw[u][1]
+            g_tile = stage.tile([P, 4 * UNIT], BF16, name="grouped", align_bytes=64)
             if kind == "q":
-                g_tile = stage.tile([P, 2 * 4 * P], BF16, name="grouped", align_bytes=64)
-                for g in range(2):
-                    d = g_tile[:, g * 4 * P:(g + 1) * 4 * P]
-                    interleave(nc.scalar.copy, d, raw_q[a][:, g, :, :], 0, P)
+                for i in range(2 * LAST):
+                    copy = nc.vector.tensor_copy if (a, i) == (NB - 1, 3) else nc.scalar.copy
+                    interleave(copy, g_tile[:, i * 4 * P:(i + 1) * 4 * P], view[:, i, :, :])
             else:
-                g_tile = stage.tile([P, 4 * UNIT], BF16, name="grouped", align_bytes=64)
-                if kind == "x":
-                    cut = UNIT - X_VEC
-                    interleave(nc.scalar.copy, g_tile[:], raw_x[a], 0, cut)
-                    interleave(nc.vector.tensor_copy, g_tile[:], raw_x[a], cut, UNIT)
-                elif kind == "w2":
-                    cut = UNIT - W2_VEC
-                    interleave(nc.scalar.copy, g_tile[:], raw_w2[a][:, b, :, :], 0, cut)
-                    interleave(nc.vector.tensor_copy, g_tile[:], raw_w2[a][:, b, :, :], cut, UNIT)
-                else:
-                    src = raw_w1[a][:, :, b * UNIT:(b + 1) * UNIT].rearrange("p j (m t) -> p m j t", t=4)
+                share = 512 if kind == "x" else 768 if kind == "w1" else (512, 1024)[a % 2]
+                if kind == "w1":
                     dst = g_tile[:].rearrange("p (t m j) -> p m j t", t=4, j=4)
-                    cut = P - W1_VEC
-                    nc.scalar.copy(out=dst[:, :cut, :, :], in_=src[:, :cut, :, :])
-                    nc.vector.tensor_copy(out=dst[:, cut:, :, :], in_=src[:, cut:, :, :])
+                    src = view.rearrange("p j (m t) -> p m j t", t=4)
+                    cut = P - share // 16
+                    if cut > 0:
+                        nc.scalar.copy(out=dst[:, :cut, :, :], in_=src[:, :cut, :, :])
+                    if cut < P:
+                        nc.vector.tensor_copy(out=dst[:, cut:, :, :], in_=src[:, cut:, :, :])
+                else:
+                    cut = UNIT - share // 4
+                    if cut > 0:
+                        interleave(nc.scalar.copy, g_tile[:, :4 * cut], view[:, :, :cut])
+                    if cut < UNIT:
+                        interleave(nc.vector.tensor_copy, g_tile[:, 4 * cut:], view[:, :, cut:])
             grouped[u] = g_tile
 
         def quantise_unit(u):
@@ -121,14 +135,15 @@ def tile_routed_moe_kernel(tc, xT, w1, w2, gate, offs, out):
                 cols = slice(a * UNIT, (a + 1) * UNIT)
                 nc.vector.quantize_mx(out=x_words[:, cols].bitcast(FP8X4), scales=x_bytes[:, cols], in_=grouped[u][:])
                 return
-            width = 2 * P if kind == "q" else UNIT
-            words = codes.tile([P, width], U32, name="words", align_bytes=64)
-            scales = codes.tile([P, width], U8, name="scales", align_bytes=64)
-            nc.vector.quantize_mx(out=words[:].bitcast(FP8X4), scales=scales[:], in_=grouped[u][:])
+            words = codes.tile([P, UNIT], U32, name="words", align_bytes=64)
+            scales = codes.tile([P, UNIT], U8, name="scales", align_bytes=64)
+            width = 2 * LAST * P if kind == "q" else UNIT
+            nc.vector.quantize_mx(out=words[:, :width].bitcast(FP8X4), scales=scales[:, :width], in_=grouped[u][:, :4 * width])
             quantised[u] = (words, scales)
 
-        def mx(dst, weights, cols, right, right_scale, start, stop):
+        def mx(dst, weights, block, right, right_scale, start, stop):
             words, scales = weights
+            cols = slice(block * P, (block + 1) * P)
             nc.tensor.matmul_mx(out=dst, lhsT=words[:, cols].bitcast(FP8X4), lhsT_scale=scales[:, cols],
                                 rhs=right.bitcast(FP8X4), rhs_scale=right_scale, start=start, stop=stop)
 
@@ -142,26 +157,40 @@ def tile_routed_moe_kernel(tc, xT, w1, w2, gate, offs, out):
                 acc = psum_h.tile([P, 4, C], F32, name="acc_h")
                 slots = slice(a * C, (a + 1) * C)
                 for t in range(4):
-                    mx(acc[:, t, :], quantised[u], slice(t * P, (t + 1) * P), s_words[:, slots], s_bytes[:, slots], True, True)
+                    mx(acc[:, t, :], quantised[u], t, s_words[:, slots], s_bytes[:, slots], True, True)
                 h = hidden.tile([P, C, 4], BF16, name="h", align_bytes=64)
-                nc.scalar.activation(out=h[:], in_=acc[:].rearrange("p t s -> p s t"), func=RELU)
+                zero = token(u, 0)
+                if zero is not None:
+                    nc.scalar.activation(out=h[:], in_=acc[:].rearrange("p t s -> p s t"), func=RELU, bias=zero[:])
+                else:
+                    nc.scalar.activation(out=h[:], in_=acc[:].rearrange("p t s -> p s t"), func=RELU)
                 hid[u] = h
             elif kind == "w2" and b == 1:
                 acc = psum_y.tile([P, NB, C], F32, name="acc_y")
                 for n in range(NB):
                     for g in range(2):
                         hw, hs = h_codes[a, g]
-                        mx(acc[:, n, :], quantised["w2", a, g], slice(n * P, (n + 1) * P), hw[:], hs[:], g == 0, g == 1)
+                        mx(acc[:, n, :], quantised["w2", a, g], n, hw[:], hs[:], g == 0, g == 1)
                 sums[u] = acc
             elif kind == "q":
-                acc = psum_y.tile([P, C], F32, name="acc_y")
-                for g in range(2):
-                    hw, hs = h_codes[E - 1, g]
-                    mx(acc[:], quantised[u], slice(g * P, (g + 1) * P), hw[:], hs[:], g == 0, g == 1)
+                acc = psum_y.tile([P, LAST, C], F32, name="acc_y")
+                for e in range(LAST):
+                    for g in range(2):
+                        hw, hs = h_codes[E - LAST + e, g]
+                        mx(acc[:, e, :], quantised[u], 2 * e + g, hw[:], hs[:], g == 0, g == 1)
                 sums[u] = acc
 
-        def scatter(b, k):
-            nc.vector.tensor_tensor(windows[b][:].indirect(lists[:, k * CUT // 16:(k + 1) * CUT // 16]), y[:, b, k * CUT:(k + 1) * CUT], gates[:, b, k * CUT:(k + 1) * CUT], MULT)
+        def empty(n, cols, src, zero):
+            dst = y[:, n, cols]
+            if zero is not None:
+                nc.scalar.activation(out=dst, in_=src, func=IDENTITY, bias=zero[:])
+            else:
+                nc.scalar.copy(out=dst, in_=src)
+
+        def scatter(n, k):
+            window = windows[n][:].indirect(lists[:, k * CUT // 16:(k + 1) * CUT // 16])
+            part = slice(k * CUT, (k + 1) * CUT)
+            nc.vector.tensor_tensor(window, y[:, n, part], gates[:, n, part], MULT)
 
         def finish_unit(u):
             kind, a, b = u
@@ -171,58 +200,34 @@ def tile_routed_moe_kernel(tc, xT, w1, w2, gate, offs, out):
                 nc.vector.quantize_mx(out=hw[:].bitcast(FP8X4), scales=hs[:], in_=hid[u][:].rearrange("p s t -> p (s t)"))
                 h_codes[a, b] = (hw, hs)
             elif kind == "w2" and b == 1:
-                slots = slice(a * C, (a + 1) * C)
-                nc.scalar.copy(out=y[:, :, slots], in_=sums[u][:])
+                later = (2, 3, 4, 5) if a % 2 else None
+                cols = slice(a * C, (a + 1) * C)
+                if later:
+                    for n in range(NB):
+                        empty(n, cols, sums[u][:, n, :], token(u, later[n]))
+                else:
+                    empty(slice(0, NB), cols, sums[u][:], None)
                 for k in range(S // CUT):
                     if a * C < (k + 1) * CUT <= (a + 1) * C:
                         for n in range(NB):
                             scatter(n, k)
             elif kind == "q":
-                slots = slice(S - C, S)
-                nc.scalar.copy(out=y[:, a, slots], in_=sums[u][:])
+                empty(a, slice(S - LAST * C, S), sums[u][:].rearrange("p e c -> p (e c)"), None)
                 scatter(a, S // CUT - 1)
                 nc.sync.dma_start(out[a * P:(a + 1) * P, :], windows[a][:])
 
-        units = [("x", c, 0) for c in range(T // UNIT)]
-        items = [(load_x, c) for c in range(T // UNIT)]
-        for e in range(E):
-            items.append((load_w1, e))
-            units.extend([("w1", e, 0), ("w1", e, 1)])
-            if e < E - 1:
-                items.append((load_w2, e))
-                units.extend([("w2", e, 0), ("w2", e, 1)])
-        items.extend([(load_q, b) for b in range(NB)])
-        units.extend([("q", b, 0) for b in range(NB)])
-
         issued = 0
-
-        def issue(upto):
-            done = issued
-            while done < min(upto, len(items)):
-                load, arg = items[done]
-                load(arg)
-                done += 1
-                if done == 4:
-                    nc.sync.dma_start(gates[:], gate_view)
-            return done
-
-        first_item = {}
-        for u in units:
-            if u[0] == "x":
-                first_item[u] = u[1]
-            elif u[0] == "q":
-                first_item[u] = len(items) - NB + u[1]
-            else:
-                first_item[u] = 3 + 2 * u[1] + (0 if u[0] == "w1" else 1)
-        AHEAD = 5
-        for step in range(len(units) + 3):
-            if step < len(units):
-                issued = issue(first_item[units[step]] + AHEAD)
+        for step in range(-1, len(units) + 3):
             if 3 <= step:
                 finish_unit(units[step - 3])
             if 2 <= step < len(units) + 2:
                 multiply_unit(units[step - 2])
             if 1 <= step < len(units) + 1:
                 quantise_unit(units[step - 1])
-            if step < len(units):
+            if 0 <= step < len(units):
                 copy_unit(units[step])
+            while issued < len(units) and issued <= step + AHEAD:
+                load(units[issued])
+                issued += 1
+                if issued == 5:
+                    nc.sync.dma_start(gates[:], gate_view)

@@ -109,10 +109,10 @@ def tile_routed_moe_kernel(tc, xT, w1, w2, gate, offs, out):
             g_tile = stage.tile([P, 4 * UNIT], BF16, name="grouped", align_bytes=64)
             if kind == "q":
                 for i in range(2 * LAST):
-                    copy = nc.vector.tensor_copy if (a, i) == (NB - 1, 3) else nc.scalar.copy
+                    copy = nc.vector.tensor_copy if False else nc.scalar.copy
                     interleave(copy, g_tile[:, i * 4 * P:(i + 1) * 4 * P], view[:, i, :, :])
             else:
-                share = 512 if kind == "x" else 768 if kind == "w1" else (512, 1024)[a % 2]
+                share = 512 if kind == "x" else (256 if a < E - LAST else 768) if kind == "w1" else (0, 1024)[a % 2]
                 if kind == "w1":
                     dst = g_tile[:].rearrange("p (t m j) -> p m j t", t=4, j=4)
                     src = view.rearrange("p j (m t) -> p m j t", t=4)

import concourse.mybir as mybir

F32 = mybir.dt.float32
BF16 = mybir.dt.bfloat16
U32 = mybir.dt.uint32
U16 = mybir.dt.uint16
U8 = mybir.dt.uint8
FP8X4 = mybir.dt.float8_e4m3fn_x4
RELU = mybir.ActivationFunctionType.Relu
IDENTITY = mybir.ActivationFunctionType.Identity
MULT = mybir.AluOpType.mult
ADD = mybir.AluOpType.add
MAX = mybir.AluOpType.max
MIN = mybir.AluOpType.min

P = 128
K, T, E, C, H, N = 512, 1536, 6, 128, 1024, 512
S = E * C
FLOPS = 2 * S * (K * H + H * N)

UNIT = 512
AHEAD = 11
LAST = 2
CUT = 256
NB = N // P


def tile_routed_moe_kernel(tc, xT, w1, w2, gate, offs, out):
    nc = tc.nc
    x_view = xT.rearrange("(p j) t -> p j t", j=4)
    w1_view = w1.rearrange("e (p j) i -> e p j i", j=4)
    w2_view = w2.rearrange("e (g p j) n -> e g p (j n)", g=2, j=4)
    w2_rows = w2.rearrange("e (g p j) n -> e g p j n", g=2, j=4)
    gate_view = gate.rearrange("(b p) s -> p b s", p=P)

    with (
        tc.tile_pool(name="keep", bufs=1) as keep,
        tc.tile_pool(name="ring", bufs=AHEAD) as ring,
        tc.tile_pool(name="stage", bufs=8) as stage,
        tc.tile_pool(name="codes", bufs=9) as codes,
        tc.tile_pool(name="hidden", bufs=3) as hidden,
        tc.tile_pool(name="tokens", bufs=16) as tokens,
        tc.psum_pool(name="psum_h", bufs=4) as psum_h,
        tc.psum_pool(name="psum_y", bufs=4) as psum_y,
    ):
        lists = keep.tile([P, S // 16], U16, name="lists")
        x_words = keep.tile([P, T], U32, name="x_words", align_bytes=64)
        x_bytes = keep.tile([P, T], U8, name="x_bytes", align_bytes=64)
        s_words = keep.tile([P, S], U32, name="s_words", align_bytes=64)
        s_bytes = keep.tile([P, S], U8, name="s_bytes", align_bytes=64)
        gates = keep.tile([P, NB, S], F32, name="gates")
        y = keep.tile([P, NB, S], F32, name="y")
        windows = []
        for b in range(NB):
            window = keep.tile([P, T], F32, name="window%d" % b)
            windows.append(window)

        nc.sync.dma_start(lists[:], offs)
        for b in range(NB):
            engine = nc.gpsimd
            engine.memset(windows[b][:], 0.0)

        raw = {}
        grouped = {}
        quantised = {}
        sums = {}
        hid = {}
        h_codes = {}

        units = [("x", c, 0) for c in range(T // UNIT)]
        for e in range(E):
            units.extend([("w1", e, 0), ("w1", e, 1)])
            if e < E - LAST:
                units.extend([("w2", e, 0), ("w2", e, 1)])
        units.extend([("q", b, 0) for b in range(NB)])

        def load(u):
            kind, a, b = u
            tile = ring.tile([P, 4 * UNIT], F32, name="raw")
            if kind == "q":
                view = tile[:, :2 * LAST * 4 * P].rearrange("p (i j n) -> p i j n", i=2 * LAST, j=4)
                for i in range(2 * LAST):
                    e, g = divmod(i, 2)
                    nc.sync.dma_start(view[:, i, :, :], w2_rows[E - LAST + e, g, :, :, a * P:(a + 1) * P])
            else:
                view = tile[:].rearrange("p (j c) -> p j c", j=4)
                if kind == "x":
                    nc.sync.dma_start(view, x_view[:, :, a * UNIT:(a + 1) * UNIT])
                elif kind == "w1":
                    nc.sync.dma_start(view, w1_view[a, :, :, b * UNIT:(b + 1) * UNIT])
                else:
                    nc.sync.dma_start(tile[:], w2_view[a, b, :, :])
            raw[u] = (tile, view)

        def token(u, later):
            at = units.index(u) + later
            if later == 0 or at >= len(units):
                return None
            zero = tokens.tile([P, 1], F32, name="zero")
            nc.gpsimd.tensor_scalar(out=zero[:], in0=raw[units[at]][0][:, 0:1], scalar1=0.0, scalar2=0.0, op0=MAX, op1=MIN)
            return zero

        def interleave(copy, dst, src):
            copy(out=dst.rearrange("p (c i j) -> p c j i", i=4, j=4), in_=src.rearrange("p j (c i) -> p c j i", i=4))

        def copy_unit(u):
            kind, a, b = u
            view = raw[u][1]
            g_tile = stage.tile([P, 4 * UNIT], BF16, name="grouped", align_bytes=64)
            if kind == "q":
                for i in range(2 * LAST):
                    copy = nc.vector.tensor_copy if False else nc.scalar.copy
                    interleave(copy, g_tile[:, i * 4 * P:(i + 1) * 4 * P], view[:, i, :, :])
            else:
                share = 512 if kind == "x" else (256 if a < E - LAST else 768) if kind == "w1" else (0, 1024)[a % 2]
                if kind == "w1":
                    dst = g_tile[:].rearrange("p (t m j) -> p m j t", t=4, j=4)
                    src = view.rearrange("p j (m t) -> p m j t", t=4)
                    cut = P - share // 16
                    if cut > 0:
                        nc.scalar.copy(out=dst[:, :cut, :, :], in_=src[:, :cut, :, :])
                    if cut < P:
                        nc.vector.tensor_copy(out=dst[:, cut:, :, :], in_=src[:, cut:, :, :])
                else:
                    cut = UNIT - share // 4
                    if cut > 0:
                        interleave(nc.scalar.copy, g_tile[:, :4 * cut], view[:, :, :cut])
                    if cut < UNIT:
                        interleave(nc.vector.tensor_copy, g_tile[:, 4 * cut:], view[:, :, cut:])
            grouped[u] = g_tile

        def quantise_unit(u):
            kind, a, b = u
            if kind == "x":
                cols = slice(a * UNIT, (a + 1) * UNIT)
                nc.vector.quantize_mx(out=x_words[:, cols].bitcast(FP8X4), scales=x_bytes[:, cols], in_=grouped[u][:])
                return
            words = codes.tile([P, UNIT], U32, name="words", align_bytes=64)
            scales = codes.tile([P, UNIT], U8, name="scales", align_bytes=64)
            width = 2 * LAST * P if kind == "q" else UNIT
            nc.vector.quantize_mx(out=words[:, :width].bitcast(FP8X4), scales=scales[:, :width], in_=grouped[u][:, :4 * width])
            quantised[u] = (words, scales)

        def mx(dst, weights, block, right, right_scale, start, stop):
            words, scales = weights
            cols = slice(block * P, (block + 1) * P)
            nc.tensor.matmul_mx(out=dst, lhsT=words[:, cols].bitcast(FP8X4), lhsT_scale=scales[:, cols],
                                rhs=right.bitcast(FP8X4), rhs_scale=right_scale, start=start, stop=stop)

        def multiply_unit(u):
            kind, a, b = u
            if kind == "x":
                if a == T // UNIT - 1:
                    nc.vector.tensor_copy(s_words[:], x_words[:].indirect(lists[:]))
                    nc.vector.tensor_copy(s_bytes[:], x_bytes[:].indirect(lists[:]))
            elif kind == "w1":
                acc = psum_h.tile([P, 4, C], F32, name="acc_h")
                slots = slice(a * C, (a + 1) * C)
                for t in range(4):
                    mx(acc[:, t, :], quantised[u], t, s_words[:, slots], s_bytes[:, slots], True, True)
                h = hidden.tile([P, C, 4], BF16, name="h", align_bytes=64)
                zero = token(u, 0)
                if zero is not None:
                    nc.scalar.activation(out=h[:], in_=acc[:].rearrange("p t s -> p s t"), func=RELU, bias=zero[:])
                else:
                    nc.scalar.activation(out=h[:], in_=acc[:].rearrange("p t s -> p s t"), func=RELU)
                hid[u] = h
            elif kind == "w2" and b == 1:
                acc = psum_y.tile([P, NB, C], F32, name="acc_y")
                for n in range(NB):
                    for g in range(2):
                        hw, hs = h_codes[a, g]
                        mx(acc[:, n, :], quantised["w2", a, g], n, hw[:], hs[:], g == 0, g == 1)
                sums[u] = acc
            elif kind == "q":
                acc = psum_y.tile([P, LAST, C], F32, name="acc_y")
                for e in range(LAST):
                    for g in range(2):
                        hw, hs = h_codes[E - LAST + e, g]
                        mx(acc[:, e, :], quantised[u], 2 * e + g, hw[:], hs[:], g == 0, g == 1)
                sums[u] = acc

        def empty(n, cols, src, zero):
            dst = y[:, n, cols]
            if zero is not None:
                nc.scalar.activation(out=dst, in_=src, func=IDENTITY, bias=zero[:])
            else:
                nc.scalar.copy(out=dst, in_=src)

        def scatter(n, k):
            window = windows[n][:].indirect(lists[:, k * CUT // 16:(k + 1) * CUT // 16])
            part = slice(k * CUT, (k + 1) * CUT)
            nc.vector.tensor_tensor(window, y[:, n, part], gates[:, n, part], MULT)

        def finish_unit(u):
            kind, a, b = u
            if kind == "w1":
                hw = hidden.tile([P, C], U32, name="h_words%d" % b, align_bytes=64)
                hs = hidden.tile([P, C], U8, name="h_scales%d" % b, align_bytes=64)
                nc.vector.quantize_mx(out=hw[:].bitcast(FP8X4), scales=hs[:], in_=hid[u][:].rearrange("p s t -> p (s t)"))
                h_codes[a, b] = (hw, hs)
            elif kind == "w2" and b == 1:
                later = (2, 3, 4, 5) if a % 2 else None
                cols = slice(a * C, (a + 1) * C)
                if later:
                    for n in range(NB):
                        empty(n, cols, sums[u][:, n, :], token(u, later[n]))
                else:
                    empty(slice(0, NB), cols, sums[u][:], None)
                for k in range(S // CUT):
                    if a * C < (k + 1) * CUT <= (a + 1) * C:
                        for n in range(NB):
                            scatter(n, k)
            elif kind == "q":
                empty(a, slice(S - LAST * C, S), sums[u][:].rearrange("p e c -> p (e c)"), None)
                scatter(a, S // CUT - 1)
                nc.sync.dma_start(out[a * P:(a + 1) * P, :], windows[a][:])

        issued = 0
        for step in range(-1, len(units) + 3):
            if 3 <= step:
                finish_unit(units[step - 3])
            if 2 <= step < len(units) + 2:
                multiply_unit(units[step - 2])
            if 1 <= step < len(units) + 1:
                quantise_unit(units[step - 1])
            if 0 <= step < len(units):
                copy_unit(units[step])
            while issued < len(units) and issued <= step + AHEAD:
                load(units[issued])
                issued += 1
                if issued == 5:
                    nc.sync.dma_start(gates[:], gate_view)
